import numpy as np
import ml_dtypes


def mxq(x, axis, fmt="e4m3"):
    dtype, down = {"e4m3": (ml_dtypes.float8_e4m3fn, 7), "e5m2": (ml_dtypes.float8_e5m2, 14)}[fmt]
    v = np.moveaxis(np.asarray(x, np.float32).astype(ml_dtypes.bfloat16).astype(np.float64), axis, -1)
    blocks = v.reshape(v.shape[:-1] + (-1, 32))
    amax = np.abs(blocks).max(-1, keepdims=True)
    byte = np.maximum(np.where(amax > 0, np.frexp(amax)[1] - 1 + 127, 0) - down, 1)
    scale = np.exp2(byte - 127.0)
    codes = (blocks / scale).astype(np.float32).astype(dtype).astype(np.float64)
    return np.moveaxis((codes * scale).reshape(v.shape), -1, axis)


WIDE = False


def mx_kscale(k):
    if not WIDE:
        return np.ones(k)
    levels = np.array([10, -10, 5, -5, 0])
    if k % 512:
        return np.exp2(np.random.permutation(np.resize(levels, k // 32))).repeat(32)
    a = np.empty((k // 512, 16))
    for p in range(k // 512):
        a[p, :8] = np.random.permutation(np.resize(levels, 8))
        for g in range(8):
            far = levels[np.abs(levels - a[p, g]) >= 10]
            a[p, g + 8] = far[np.random.randint(len(far))]
    return np.exp2(a.ravel()).repeat(32)


def f64(x):
    return np.asarray(x).astype(np.float64)


def striped(idx):
    return np.tile(idx.reshape(-1, 16).T, (8, 1)).astype(np.uint16)


def unstriped(offs):
    return offs[:16].T.reshape(-1).astype(np.int64)


E2M1 = np.array([0.0, 0.5, 1.0, 1.5, 2.0, 3.0, 4.0, 6.0, -0.0, -0.5, -1.0, -1.5, -2.0, -3.0, -4.0, -6.0])


def pack_weight(w, fmt):
    k, n = w.shape
    w = f64(np.asarray(w, np.float32).astype(ml_dtypes.bfloat16)).reshape(k // 32, 32, n)
    amax = np.abs(w).max(1)
    if fmt == "e4m3":
        byte = np.frexp(amax)[1] - 1 + 127 - 7
    else:
        mant, ex = np.frexp(amax / 6.0)
        byte = np.where(mant > 0.5, ex, ex - 1) + 127
    byte = np.clip(np.where(amax > 0, byte, 1), 1, 254)
    scaled = (w * np.exp2(127.0 - byte)[:, None, :]).reshape(k, n).astype(np.float32)
    by_word = np.ascontiguousarray(scaled.reshape(k // 512, 128, 4, n).transpose(0, 1, 3, 2))
    if fmt == "e4m3":
        words = by_word.astype(ml_dtypes.float8_e4m3fn).view(np.uint8)
    else:
        c = by_word.astype(ml_dtypes.float4_e2m1fn).view(np.uint8) & 0xF
        words = (c[..., 0::2] | (c[..., 1::2] << 4)).reshape(k // 512, 128, 2 * n)
    return np.ascontiguousarray(words), np.ascontiguousarray(byte.astype(np.uint8).reshape(k // 512, 16, n))


def unpack_weight(words, scales, fmt):
    g, _, n = scales.shape
    words = np.ascontiguousarray(words).reshape(g, 128, n, -1)
    if fmt == "e4m3":
        vals = words.view(ml_dtypes.float8_e4m3fn).astype(np.float64)
    else:
        nib = np.empty((g, 128, n, 4), np.uint8)
        nib[..., 0::2] = words & 0xF
        nib[..., 1::2] = words >> 4
        vals = E2M1[nib]
    vals = vals * np.repeat(np.exp2(scales.astype(np.float64) - 127.0), 8, axis=1)[..., None]
    return vals.transpose(0, 1, 3, 2).reshape(g * 512, n)


def gelu(v):
    return 0.5 * v * (1.0 + np.tanh(np.sqrt(2.0 / np.pi) * (v + 0.044715 * v**3)))


K, H, T, S, T2, T3, S2, P = 1024, 1024, 2048, 512, 1024, 2048, 512, 512

def setup_inputs():
    n = np.random.standard_normal
    s = mx_kscale(K)[:, None]
    u = mx_kscale(H)[:, None]
    tab_words, tab_scales = pack_weight(n((K, T)) * s, "e4m3")
    tab2_words, tab2_scales = pack_weight(n((H, T3)) / u / np.sqrt(H), "e4m3")
    w4_words, w4_scales = pack_weight(n((K, H)) / s / np.sqrt(K), "e2m1")
    w8_words, w8_scales = pack_weight(0.7 * n((K, H)) / s * u.T / np.sqrt(K), "e4m3")
    return {
        "tab_words": tab_words, "tab_scales": tab_scales,
        "tab2_words": tab2_words, "tab2_scales": tab2_scales,
        "w4_words": w4_words, "w4_scales": w4_scales,
        "w8_words": w8_words, "w8_scales": w8_scales,
        "w1": (n((K, H)) / s * u.T / np.sqrt(K)).astype(np.float32),
        "page0": (n((H, T2)) * u).astype(np.float32),
        "wgs": np.exp(0.3 * n((128, S))).astype(np.float32),
        "budget": np.random.uniform(0.5, 2.0, S2).astype(np.float32),
        "offs": striped(np.random.permutation(T)[:S]),
        "offs2": striped(np.random.permutation(T3)[:S2]),
        "offs3": striped(np.random.permutation(T2)[:S]),
        "offs4": striped(np.random.permutation(T2)[:P]),
    }

def reference(tab_words, tab_scales, tab2_words, tab2_scales, w4_words, w4_scales,
              w8_words, w8_scales, w1, page0, wgs, budget, offs, offs2, offs3, offs4):
    v = unpack_weight(tab_words, tab_scales, "e4m3")[:, unstriped(offs)]
    v2 = unpack_weight(tab2_words, tab2_scales, "e4m3")[:, unstriped(offs2)]
    gate = unpack_weight(w4_words, w4_scales, "e2m1").T @ v
    val = mxq(f64(w1), 0, "e4m3").T @ v
    skip = unpack_weight(w8_words, w8_scales, "e4m3").T @ v
    h = gate / (1.0 + np.exp(-gate)) * val + skip
    page = f64(page0).copy()
    page[:, unstriped(offs3)] = np.tile(f64(wgs), (H // 128, 1)) * h
    e = v2.T @ mxq(page, 0, "e4m3")
    x = e[:, unstriped(offs4)]
    return np.log(1.0 + np.square(f64(budget)[:, None] * x))

@@ -1,0 +1,339 @@
+from contextlib import ExitStack
+
+import concourse.mybir as mybir
+from concourse.masks import make_identity
+
+K, H, T, S, T2, T3, S2, NP = 1024, 1024, 2048, 512, 1024, 2048, 512, 512
+FLOPS = 2 * 3 * K * H * S + 2 * H * S2 * T2
+
+F32 = mybir.dt.float32
+BF16 = mybir.dt.bfloat16
+I32 = mybir.dt.int32
+U32 = mybir.dt.uint32
+U16 = mybir.dt.uint16
+U8 = mybir.dt.uint8
+FP8X4 = mybir.dt.float8_e4m3fn_x4
+FP4X4 = mybir.dt.float4_e2m1fn_x4
+ACT = mybir.ActivationFunctionType
+MULT = mybir.AluOpType.mult
+
+P = 128
+PACK = 4
+KP = P * PACK
+PER_COL = 16
+SPLIT = 640
+
+
+def tile_list_sponsor_slot_scores_kernel(
+    tc, tab_words, tab_scales, tab2_words, tab2_scales, w4_words, w4_scales,
+    w8_words, w8_scales, w1, page0, wgs, budget, offs, offs2, offs3, offs4, out,
+):
+    nc = tc.nc
+    with ExitStack() as ctx:
+        held = ctx.enter_context(tc.tile_pool(name="held", bufs=1))
+        ring = ctx.enter_context(tc.tile_pool(name="ring", bufs=4))
+        psum = ctx.enter_context(tc.psum_pool(name="psum", bufs=1))
+
+        def keep(name, shape, dtype, tag=None):
+            return held.tile(shape, dtype, name=name, tag=tag or name, align_bytes=64)
+
+        def entries(lst, lo, hi):
+            return lst[:, lo // PER_COL : hi // PER_COL]
+
+        idx = keep("idx", [P, S // PER_COL], U16)
+        idx2 = keep("idx2", [P, S2 // PER_COL], U16)
+        idx3 = keep("idx3", [P, S // PER_COL], U16)
+        idx4 = keep("idx4", [P, NP // PER_COL], U16)
+
+        tab_sc = keep("tab_sc", [P, 2 * T], U8)
+        tab2_sc = keep("tab2_sc", [P, T3], U8)
+        w4_sc = keep("w4_sc", [P, 2 * H], U8)
+        w8_sc = keep("w8_sc", [P, H], U8)
+        nc.vector.memset(tab_sc[:].bitcast(I32), 0)
+        nc.vector.memset(tab2_sc[:].bitcast(I32), 0)
+        nc.gpsimd.memset(w4_sc[:].bitcast(I32), 0)
+        nc.gpsimd.memset(w8_sc[:].bitcast(I32), 0)
+
+        def load_planes_side_by_side(queue, dst, scales):
+            for q in range(4):
+                queue.dma_start(
+                    dst[32 * q : 32 * q + 4, :].bitcast(I32).rearrange("r (a n) -> r a n", a=2),
+                    scales[:, 4 * q : 4 * q + 4, :].bitcast(I32).rearrange("a r n -> r a n"),
+                )
+
+        def load_planes_stacked(dst, scales):
+            for q in range(4):
+                nc.gpsimd.dma_start(
+                    dst[32 * q : 32 * q + 8, :].bitcast(I32),
+                    scales[:, 4 * q : 4 * q + 4, :].bitcast(I32),
+                )
+
+        def load_words(dst, words):
+            nc.sync.dma_start(dst[:].bitcast(I32), words.rearrange("p n i -> p (n i)").bitcast(I32))
+
+        w1_raw = [[keep(f"w1_raw{a}{b}", [P, PACK, KP], F32) for b in range(2)] for a in range(2)]
+        w4 = [keep(f"w4_{b}", [P, 2, 2 * KP], U8) for b in range(2)]
+        w8 = [keep(f"w8_{b}", [P, 2, KP], U32) for b in range(2)]
+        tab = [keep(f"tab{a}", [P, T], U32) for a in range(2)]
+        tab2 = [keep(f"tab2_{a}", [P, T3], U32) for a in range(2)]
+        page = [[keep(f"page{b}{t}", [P, T2], F32) for t in range(PACK)] for b in range(2)]
+        gain = keep("gain", [P, PACK * S], F32)
+        budget_col = keep("budget_col", [P, S2 // P], F32)
+
+        def load_w1(a, b):
+            rows = w1[KP * a : KP * (a + 1), KP * b : KP * (b + 1)]
+            nc.sync.dma_start(w1_raw[a][b][:], rows.rearrange("(p i) c -> p i c", i=PACK))
+
+        def load_w4(b):
+            nc.sync.dma_start(
+                w4[b][:].bitcast(I32),
+                w4_words.rearrange("a p n -> p a n")[:, :, 2 * KP * b : 2 * KP * (b + 1)].bitcast(I32),
+            )
+
+        def load_w8(b):
+            nc.sync.dma_start(
+                w8[b][:].bitcast(I32),
+                w8_words.rearrange("a p n i -> p a (n i)")[:, :, 4 * KP * b : 4 * KP * (b + 1)].bitcast(I32),
+            )
+
+        def load_page(b, t):
+            nc.sync.dma_start(page[b][t][:], page0.rearrange("(b p t) n -> b t p n", b=2, t=PACK)[b, t])
+
+        def load_gain():
+            rows = wgs.rearrange("(q t) j -> q (t j)", t=PACK)
+            for q in range(4):
+                nc.sync.dma_start(gain[32 * q : 32 * (q + 1), :], rows)
+
+        ident = keep("ident", [P, P], F32)
+        make_identity(nc, ident[:])
+        load_planes_side_by_side(nc.gpsimd, w4_sc, w4_scales)
+        load_planes_stacked(w8_sc, w8_scales)
+        load_planes_stacked(tab2_sc, tab2_scales)
+        load_w1(0, 0)
+        load_w1(1, 0)
+        for dst, lst in ((idx, offs), (idx2, offs2), (idx3, offs3), (idx4, offs4)):
+            nc.sync.dma_start(dst[:], lst)
+        load_words(tab[0], tab_words[0])
+        load_w4(0)
+        load_planes_side_by_side(nc.sync, tab_sc, tab_scales)
+        load_words(tab[1], tab_words[1])
+        load_w8(0)
+        load_gain()
+        for t in range(PACK):
+            load_page(0, t)
+        load_w1(0, 1)
+        load_w1(1, 1)
+        load_w4(1)
+        load_w8(1)
+        load_page(1, 0)
+        load_words(tab2[0], tab2_words[0])
+        load_words(tab2[1], tab2_words[1])
+        for t in range(1, PACK):
+            load_page(1, t)
+        with nc.allow_non_contiguous_dma(reason="one budget value a partition"):
+            nc.sync.dma_start(budget_col[:], budget.rearrange("(c p) -> p c", p=P))
+
+        w1_bf = [[keep(f"w1_bf{a}0", [P, KP * PACK], BF16)[:], None] for a in range(2)]
+        w1_q = [[keep(f"w1_q{a}{b}", [P, KP], U32) for b in range(2)] for a in range(2)]
+        w1_sc = [[keep(f"w1_sc{a}{b}", [P, KP], U8) for b in range(2)] for a in range(2)]
+
+        def interleave(copy, dst, src):
+            copy(dst.rearrange("p (c n i) -> p c i n", n=4, i=PACK), src.rearrange("p i (c n) -> p c i n", n=4))
+
+        def quantise(codes, scales, values):
+            nc.vector.quantize_mx(out=codes[:].bitcast(FP8X4), scales=scales[:], in_=values)
+
+        picked = [keep(f"picked{a}", [P, S], U32) for a in range(2)]
+        picked_sc = [keep(f"picked_sc{a}", [P, S], U8) for a in range(2)]
+
+        def pick_scales(a, lo, hi):
+            nc.vector.tensor_copy(picked_sc[a][:, lo:hi], tab_sc[:, T * a : T * (a + 1)].indirect(entries(idx, lo, hi)))
+
+        def pick_words(a, lo, hi):
+            nc.vector.tensor_copy(picked[a][:, lo:hi], tab[a][:].indirect(entries(idx, lo, hi)))
+
+        half = S // 2
+        for a in range(2):
+            interleave(nc.vector.tensor_copy, w1_bf[a][0], w1_raw[a][0][:])
+        for a in range(2):
+            quantise(w1_q[a][0], w1_sc[a][0], w1_bf[a][0])
+        pick_words(0, 0, half)
+        pick_scales(0, 0, half)
+        pick_scales(1, 0, half)
+        pick_words(0, half, S)
+        pick_words(1, 0, half)
+        pick_scales(0, half, S)
+        pick_words(1, half, S)
+        pick_scales(1, half, S)
+
+        turned = [{}, keep("turned1", [P, PACK, S], F32)]
+        made = {}
+        slots = {
+            ("lin", 0, 1): "w1_bf01", ("act", 0, 1): "cand_sc",
+            ("act", 1, 1): "cand0", ("act", 1, 0): "cand1", ("lin", 1, 0): "hold",
+        }
+
+        def by_plane(bank):
+            return bank[:].rearrange("p (c n t) -> p c t n", n=4, t=PACK)
+
+        def as_planes(tile_):
+            return tile_[:].rearrange("p (t c n) -> p c t n", t=PACK, n=4)
+
+        def first_products(b, u):
+            cols = slice(P * u, P * (u + 1))
+            n = len(made)
+            gate = psum.tile([P, KP], F32, name=f"gate{n}", tag="gate")
+            val = psum.tile([P, KP], F32, name=f"val{n}", tag="ABCDBCDB"[n])
+            skip = psum.tile([P, KP], F32, name=f"skip{n}", tag="BAEAEAEA"[n])
+
+            def product(bank, a, codes, scales):
+                nc.tensor.matmul_mx(
+                    out=bank[:], lhsT=picked[a][:, cols].bitcast(FP8X4), lhsT_scale=picked_sc[a][:, cols],
+                    rhs=codes, rhs_scale=scales, start=(a == 0), stop=(a == 1),
+                )
+
+            for a in range(2):
+                product(gate, a, w4[b][:, a, :].bitcast(FP4X4), w4_sc[:, H * a + KP * b : H * a + KP * (b + 1)])
+                product(val, a, w1_q[a][b][:].bitcast(FP8X4), w1_sc[a][b][:])
+            for a in range(2):
+                product(skip, a, w8[b][:, a, :].bitcast(FP8X4), w8_sc[4 * a :, KP * b : KP * (b + 1)])
+            def stage(kind):
+                slot = slots.get((kind, b, u))
+                if slot:
+                    return keep(kind + slot, [P, KP], F32, slot)
+                return ring.tile([P, KP], F32, name=kind, tag=kind)
+
+            act = stage("act")
+            nc.scalar.activation(as_planes(act), by_plane(gate), ACT.Silu)
+            lin = stage("lin")
+            nc.scalar.copy(as_planes(lin), by_plane(skip))
+            gated = stage("gated")
+            nc.vector.tensor_tensor(as_planes(gated), by_plane(val), as_planes(act), MULT)
+            return gated, lin
+
+        def turn(b, u, gated, lin):
+            bank = psum.tile([P, PACK, P], F32, name=f"turn{b}{u}", tag=f"turn{u % 2 if b == 0 else u // 2}")
+            for t in range(PACK):
+                cols = slice(P * t, P * (t + 1))
+                nc.tensor.matmul(bank[:, t, :], gated[:, cols], ident[:], is_transpose=True, start=True, stop=False)
+                nc.tensor.matmul(bank[:, t, :], lin[:, cols], ident[:], is_transpose=True, start=False, stop=True)
+            return bank
+
+        def drain(b, u, bank):
+            if b == 0:
+                turned[0][u] = keep(f"turned0{u}", [P, PACK, P], F32, {2: "w1_bf01", 3: "hold"}.get(u))
+            if (b, u) == (1, 0):
+                nc.scalar.copy(turned[1][:, 0:3, P * u : P * (u + 1)], bank[:, 0:3, :])
+            else:
+                nc.scalar.copy(turned[0][u][:] if b == 0 else turned[1][:, :, P * u : P * (u + 1)], bank[:])
+
+        def scatter(b, t, lo, hi, src=None):
+            if src is None:
+                src = turned[0][lo // P][:, t, :] if b == 0 else turned[1][:, t, lo:hi]
+            nc.vector.tensor_tensor(
+                page[b][t][:].indirect(entries(idx3, lo, hi)), src, gain[:, S * t + lo : S * t + hi], MULT,
+            )
+
+
+        def start(b, u):
+            made[b, u] = first_products(b, u)
+
+        def finish(b, u, bank=None):
+            if bank is None:
+                bank = turn(b, u, *made[b, u])
+            drain(b, u, bank)
+            for t in range(PACK if b == 0 else 1):
+                scatter(b, t, P * u, P * (u + 1))
+
+        def pick_candidates(a):
+            words = keep(f"cand{a}", [P, S2], U32)
+            nc.vector.tensor_copy(words[:], tab2[a][:].indirect(idx2[:]))
+            return words
+
+        start(0, 0)
+        finish(0, 0)
+        start(0, 1)
+        cand_sc = keep("cand_sc", [P, S2], U8)
+        nc.vector.tensor_copy(cand_sc[:], tab2_sc[:].indirect(idx2[:]))
+        start(0, 2)
+        finish(0, 1)
+        start(0, 3)
+        for a in range(2):
+            w1_bf[a][1] = keep(f"w1_bf{a}1", [P, KP * PACK], BF16, ("w1_bf01", "w1_raw01")[a])[:]
+            interleave(nc.scalar.copy, w1_bf[a][1], w1_raw[a][1][:])
+            quantise(w1_q[a][1], w1_sc[a][1], w1_bf[a][1])
+        finish(0, 2)
+        bank03 = turn(0, 3, *made[0, 3])
+        start(1, 1)
+        cand = [pick_candidates(0)]
+        start(1, 2)
+        finish(1, 1)
+        start(1, 0)
+        cand.append(pick_candidates(1))
+        last_bank = turn(1, 0, *made[1, 0])
+        start(1, 3)
+        finish(0, 3, bank03)
+        finish(1, 0, last_bank)
+        finish(1, 2)
+        finish(1, 3)
+        warm = keep("warm", [P, 1], F32, "tab0")
+        nc.scalar.activation(warm[:], turned[1][:, 0, S - 1 : S], ACT.Ln, bias=1.0, scale=0.0)
+
+        page_bf = [keep(f"page_bf{b}", [P, T2 * PACK], BF16, f"tab{b}") for b in range(2)]
+        page_q = [keep(f"page_q{b}", [P, T2], U32) for b in range(2)]
+        page_sc = [keep(f"page_sc{b}", [P, T2], U8) for b in range(2)]
+        joined = [keep(f"joined{c}", [P, PACK, KP], F32, f"w1_raw{c}0") for c in range(2)]
+        for c in range(2):
+            for t in range(PACK):
+                nc.sync.dma_start(joined[c][:, t, :], page[0][t][:, KP * c : KP * (c + 1)])
+
+        def round_plane(copy, t, lo, hi):
+            copy(page_bf[1][:].rearrange("p (n t) -> p n t", t=PACK)[:, lo:hi, t], page[1][t][:, lo:hi])
+
+        score = [[None, None] for m in range(4)]
+        tags = [["gate", "A"], ["E", "B"], ["C", "D"], ["turn1", "turn0"]]
+
+        def second_pass(b, m, c):
+            rows = slice(P * m, P * (m + 1))
+            if b == 0:
+                score[m][c] = psum.tile([P, KP], F32, name=f"score{m}{c}", tag=tags[m][c])
+            nc.tensor.matmul_mx(
+                out=score[m][c][:], lhsT=cand[b][:, rows].bitcast(FP8X4), lhsT_scale=cand_sc[4 * b :, rows],
+                rhs=page_q[b][:, KP * c : KP * (c + 1)].bitcast(FP8X4), rhs_scale=page_sc[b][:, KP * c : KP * (c + 1)], start=(b == 0), stop=(b == 1),
+            )
+
+        for c in range(2):
+            interleave(nc.scalar.copy, page_bf[0][:, KP * PACK * c : KP * PACK * (c + 1)], joined[c][:])
+        late = keep("late", [P, P], F32, "w1_raw10")
+        nc.scalar.copy(late[:], last_bank[:, 3, :])
+        round_plane(nc.scalar.copy, 0, 0, T2)
+        scatter(1, 1, 0, S)
+        round_plane(nc.scalar.copy, 1, 0, T2)
+        scatter(1, 2, 0, S)
+        round_plane(nc.vector.tensor_copy, 2, 0, SPLIT)
+        round_plane(nc.scalar.copy, 2, SPLIT, T2)
+        scatter(1, 3, P, S)
+        quantise(page_q[0], page_sc[0], page_bf[0][:])
+        scatter(1, 3, 0, P, late[:])
+        round_plane(nc.vector.tensor_copy, 3, 0, SPLIT)
+        round_plane(nc.scalar.copy, 3, SPLIT, T2)
+        quantise(page_q[1], page_sc[1], page_bf[1][:])
+        for m in range(4):
+            for b in range(2):
+                for c in range(2):
+                    second_pass(b, m, c)
+        for m in range(4):
+            row = keep(f"row{m}", [P, T2], F32)
+            for c in range(2):
+                copy = nc.scalar.copy if (m, c) in ((0, 0), (1, 0), (1, 1), (2, 0)) else nc.vector.tensor_copy
+                copy(row[:, KP * c : KP * (c + 1)], score[m][c][:])
+            pieces = 1 if m < 3 else 2
+            for k in range(pieces):
+                lo, hi = NP * k // pieces, NP * (k + 1) // pieces
+                unsold = ring.tile([P, hi - lo], F32, name="unsold", tag="act")
+                nc.vector.tensor_copy(unsold[:], row[:].indirect(entries(idx4, lo, hi)))
+                squared = ring.tile([P, hi - lo], F32, name="squared", tag="lin")
+                nc.scalar.activation(squared[:], unsold[:], ACT.Square, scale=budget_col[:, m : m + 1])
+                result = ring.tile([P, hi - lo], F32, name="result", tag="gated")
+                nc.scalar.activation(result[:], squared[:], ACT.Ln, bias=1.0)
+                nc.sync.dma_start(out[P * m : P * (m + 1), lo:hi], result[:])

@@ -21,7 +21,6 @@ P = 128
 PACK = 4
 KP = P * PACK
 PER_COL = 16
-SPLIT = 640
 
 
 def tile_list_sponsor_slot_scores_kernel(
@@ -31,7 +30,7 @@ def tile_list_sponsor_slot_scores_kernel(
     nc = tc.nc
     with ExitStack() as ctx:
         held = ctx.enter_context(tc.tile_pool(name="held", bufs=1))
-        ring = ctx.enter_context(tc.tile_pool(name="ring", bufs=4))
+        ring = ctx.enter_context(tc.tile_pool(name="ring", bufs=3))
         psum = ctx.enter_context(tc.psum_pool(name="psum", bufs=1))
 
         def keep(name, shape, dtype, tag=None):
@@ -48,22 +47,24 @@ def tile_list_sponsor_slot_scores_kernel(
         tab_sc = keep("tab_sc", [P, 2 * T], U8)
         tab2_sc = keep("tab2_sc", [P, T3], U8)
         w4_sc = keep("w4_sc", [P, 2 * H], U8)
-        w8_sc = keep("w8_sc", [P, H], U8)
+        w8_sc = keep("w8_sc", [P, 2 * H], U8)
         nc.vector.memset(tab_sc[:].bitcast(I32), 0)
-        nc.vector.memset(tab2_sc[:].bitcast(I32), 0)
+        ident = keep("ident", [P, P], F32)
+        make_identity(nc, ident[:])
         nc.gpsimd.memset(w4_sc[:].bitcast(I32), 0)
-        nc.gpsimd.memset(w8_sc[:].bitcast(I32), 0)
+        nc.vector.memset(w8_sc[:].bitcast(I32), 0)
+        nc.vector.memset(tab2_sc[:].bitcast(I32), 0)
 
-        def load_planes_side_by_side(queue, dst, scales):
-            for q in range(4):
+        def load_planes_side_by_side(queue, dst, scales, quadrants):
+            for q in quadrants:
                 queue.dma_start(
                     dst[32 * q : 32 * q + 4, :].bitcast(I32).rearrange("r (a n) -> r a n", a=2),
                     scales[:, 4 * q : 4 * q + 4, :].bitcast(I32).rearrange("a r n -> r a n"),
                 )
 
-        def load_planes_stacked(dst, scales):
+        def load_planes_stacked(queue, dst, scales):
             for q in range(4):
-                nc.gpsimd.dma_start(
+                queue.dma_start(
                     dst[32 * q : 32 * q + 8, :].bitcast(I32),
                     scales[:, 4 * q : 4 * q + 4, :].bitcast(I32),
                 )
@@ -99,26 +100,22 @@ def tile_list_sponsor_slot_scores_kernel(
         def load_page(b, t):
             nc.sync.dma_start(page[b][t][:], page0.rearrange("(b p t) n -> b t p n", b=2, t=PACK)[b, t])
 
-        def load_gain():
-            rows = wgs.rearrange("(q t) j -> q (t j)", t=PACK)
-            for q in range(4):
-                nc.sync.dma_start(gain[32 * q : 32 * (q + 1), :], rows)
 
-        ident = keep("ident", [P, P], F32)
-        make_identity(nc, ident[:])
-        load_planes_side_by_side(nc.gpsimd, w4_sc, w4_scales)
-        load_planes_stacked(w8_sc, w8_scales)
-        load_planes_stacked(tab2_sc, tab2_scales)
+        load_planes_side_by_side(nc.gpsimd, w4_sc, w4_scales, range(3))
+        load_planes_stacked(nc.gpsimd, tab2_sc, tab2_scales)
+        wgs_rows = keep("wgs_rows", [P, S], F32)
+        nc.sync.dma_start(wgs_rows[:], wgs)
         load_w1(0, 0)
         load_w1(1, 0)
         for dst, lst in ((idx, offs), (idx2, offs2), (idx3, offs3), (idx4, offs4)):
             nc.sync.dma_start(dst[:], lst)
         load_words(tab[0], tab_words[0])
+        load_planes_side_by_side(nc.sync, w4_sc, w4_scales, range(3, 4))
+        load_planes_side_by_side(nc.sync, tab_sc, tab_scales, range(4))
         load_w4(0)
-        load_planes_side_by_side(nc.sync, tab_sc, tab_scales)
         load_words(tab[1], tab_words[1])
         load_w8(0)
-        load_gain()
+        load_planes_side_by_side(nc.sync, w8_sc, w8_scales, range(4))
         for t in range(PACK):
             load_page(0, t)
         load_w1(0, 1)
@@ -133,6 +130,22 @@ def tile_list_sponsor_slot_scores_kernel(
         with nc.allow_non_contiguous_dma(reason="one budget value a partition"):
             nc.sync.dma_start(budget_col[:], budget.rearrange("(c p) -> p c", p=P))
 
+        flipped = psum.tile([P, 4, P], F32, name="flipped", tag="gate")
+        for u in range(4):
+            nc.tensor.matmul(flipped[:, u, :], wgs_rows[:, P * u : P * (u + 1)], ident[:], is_transpose=True, start=True, stop=True)
+        spread = [keep(f"spread{u}", [P, PACK, 4, 32], F32, f"spread{u}") for u in range(4)]
+        planes = [psum.tile([P, S], F32, name=f"gain_bank{t}", tag=("turn0", "D", "E", "B")[t]) for t in range(PACK)]
+        for u in range(4):
+            by_slot = flipped[:, u, :].rearrange("j (q t) -> j t q", t=PACK)
+            nc.scalar.copy(spread[u][:], by_slot.unsqueeze(2).to_broadcast([P, PACK, 4, 32]))
+            for t in range(PACK):
+                nc.tensor.matmul(
+                    planes[t][:, P * u : P * (u + 1)], spread[u][:, t, :, :].rearrange("j a q -> j (a q)"), ident[:],
+                    is_transpose=True, start=True, stop=True,
+                )
+        for t in range(PACK):
+            nc.scalar.copy(gain[:, S * t : S * (t + 1)], planes[t][:])
+
         w1_bf = [[keep(f"w1_bf{a}0", [P, KP * PACK], BF16)[:], None] for a in range(2)]
         w1_q = [[keep(f"w1_q{a}{b}", [P, KP], U32) for b in range(2)] for a in range(2)]
         w1_sc = [[keep(f"w1_sc{a}{b}", [P, KP], U8) for b in range(2)] for a in range(2)]
@@ -144,10 +157,11 @@ def tile_list_sponsor_slot_scores_kernel(
             nc.vector.quantize_mx(out=codes[:].bitcast(FP8X4), scales=scales[:], in_=values)
 
         picked = [keep(f"picked{a}", [P, S], U32) for a in range(2)]
-        picked_sc = [keep(f"picked_sc{a}", [P, S], U8) for a in range(2)]
+        picked_sc = {}
 
-        def pick_scales(a, lo, hi):
-            nc.vector.tensor_copy(picked_sc[a][:, lo:hi], tab_sc[:, T * a : T * (a + 1)].indirect(entries(idx, lo, hi)))
+        def pick_scales(a, lo, hi, dst):
+            picked_sc[a, lo] = dst
+            nc.vector.tensor_copy(dst, tab_sc[:, T * a : T * (a + 1)].indirect(entries(idx, lo, hi)))
 
         def pick_words(a, lo, hi):
             nc.vector.tensor_copy(picked[a][:, lo:hi], tab[a][:].indirect(entries(idx, lo, hi)))
@@ -158,19 +172,20 @@ def tile_list_sponsor_slot_scores_kernel(
         for a in range(2):
             quantise(w1_q[a][0], w1_sc[a][0], w1_bf[a][0])
         pick_words(0, 0, half)
-        pick_scales(0, 0, half)
-        pick_scales(1, 0, half)
+        for a in range(2):
+            pick_scales(a, 0, half, keep(f"picked_sc{a}", [P, half], U8)[:])
         pick_words(0, half, S)
         pick_words(1, 0, half)
-        pick_scales(0, half, S)
         pick_words(1, half, S)
-        pick_scales(1, half, S)
+        later_sc = keep("later_sc", [P, S], U8, "tab1")
+        for a in range(2):
+            pick_scales(a, half, S, later_sc[:, half * a : half * (a + 1)])
 
         turned = [{}, keep("turned1", [P, PACK, S], F32)]
         made = {}
         slots = {
-            ("lin", 0, 1): "w1_bf01", ("act", 0, 1): "cand_sc",
-            ("act", 1, 1): "cand0", ("act", 1, 0): "cand1", ("lin", 1, 0): "hold",
+            ("act", 0, 0): "cand_sc", ("lin", 0, 0): "after_turn0", ("act", 0, 2): "after_turn0", ("gated", 0, 0): "after_turn1", ("lin", 0, 2): "after_turn1", ("lin", 0, 1): "w1_bf01",
+            ("act", 1, 0): "w1_raw11", ("act", 1, 1): "cand0", ("lin", 1, 0): "hold", ("lin", 1, 2): "tab0", ("lin", 1, 3): "w4_0",
         }
 
         def by_plane(bank):
@@ -179,28 +194,43 @@ def tile_list_sponsor_slot_scores_kernel(
         def as_planes(tile_):
             return tile_[:].rearrange("p (t c n) -> p c t n", t=PACK, n=4)
 
-        def first_products(b, u):
+        def open_banks(n):
+            gate = psum.tile([P, KP], F32, name=f"gate{n}", tag={1: "turn1", 5: "D", 7: "D"}.get(n, "gate"))
+            val = psum.tile([P, KP], F32, name=f"val{n}", tag="ACDACACA"[n])
+            skip = psum.tile([P, KP], F32, name=f"skip{n}", tag="BE"[n % 2])
+            return gate, val, skip
+
+        def product(bank, u, a, codes, scales):
             cols = slice(P * u, P * (u + 1))
+            nc.tensor.matmul_mx(
+                out=bank[:], lhsT=picked[a][:, cols].bitcast(FP8X4), lhsT_scale=picked_sc[a, u // 2 * half][:, P * (u % 2) : P * (u % 2 + 1)],
+                rhs=codes, rhs_scale=scales, start=(a == 0), stop=(a == 1),
+            )
+
+        def gate_and_val(banks, b, u, a):
+            product(banks[0], u, a, w4[b][:, a, :].bitcast(FP4X4), w4_sc[:, H * a + KP * b : H * a + KP * (b + 1)])
+            product(banks[1], u, a, w1_q[a][b][:].bitcast(FP8X4), w1_sc[a][b][:])
+
+        early = [open_banks(n) for n in range(2)]
+        for u in range(2):
+            gate_and_val(early[u], 0, u, 0)
+
+        def first_products(b, u):
             n = len(made)
-            gate = psum.tile([P, KP], F32, name=f"gate{n}", tag="gate")
-            val = psum.tile([P, KP], F32, name=f"val{n}", tag="ABCDBCDB"[n])
-            skip = psum.tile([P, KP], F32, name=f"skip{n}", tag="BAEAEAEA"[n])
-
-            def product(bank, a, codes, scales):
-                nc.tensor.matmul_mx(
-                    out=bank[:], lhsT=picked[a][:, cols].bitcast(FP8X4), lhsT_scale=picked_sc[a][:, cols],
-                    rhs=codes, rhs_scale=scales, start=(a == 0), stop=(a == 1),
-                )
-
+            if n < 2:
+                banks = early[n]
+            else:
+                banks = open_banks(n)
+                gate_and_val(banks, b, u, 0)
+            gate_and_val(banks, b, u, 1)
+            gate, val, skip = banks
             for a in range(2):
-                product(gate, a, w4[b][:, a, :].bitcast(FP4X4), w4_sc[:, H * a + KP * b : H * a + KP * (b + 1)])
-                product(val, a, w1_q[a][b][:].bitcast(FP8X4), w1_sc[a][b][:])
-            for a in range(2):
-                product(skip, a, w8[b][:, a, :].bitcast(FP8X4), w8_sc[4 * a :, KP * b : KP * (b + 1)])
+                product(skip, u, a, w8[b][:, a, :].bitcast(FP8X4), w8_sc[:, H * a + KP * b : H * a + KP * (b + 1)])
+
             def stage(kind):
                 slot = slots.get((kind, b, u))
                 if slot:
-                    return keep(kind + slot, [P, KP], F32, slot)
+                    return keep(f"{kind}{b}{u}", [P, KP], F32, slot)
                 return ring.tile([P, KP], F32, name=kind, tag=kind)
 
             act = stage("act")
@@ -212,7 +242,7 @@ def tile_list_sponsor_slot_scores_kernel(
             return gated, lin
 
         def turn(b, u, gated, lin):
-            bank = psum.tile([P, PACK, P], F32, name=f"turn{b}{u}", tag=f"turn{u % 2 if b == 0 else u // 2}")
+            bank = psum.tile([P, PACK, P], F32, name=f"turn{b}{u}", tag=f"turn{u % 2}")
             for t in range(PACK):
                 cols = slice(P * t, P * (t + 1))
                 nc.tensor.matmul(bank[:, t, :], gated[:, cols], ident[:], is_transpose=True, start=True, stop=False)
@@ -222,10 +252,7 @@ def tile_list_sponsor_slot_scores_kernel(
         def drain(b, u, bank):
             if b == 0:
                 turned[0][u] = keep(f"turned0{u}", [P, PACK, P], F32, {2: "w1_bf01", 3: "hold"}.get(u))
-            if (b, u) == (1, 0):
-                nc.scalar.copy(turned[1][:, 0:3, P * u : P * (u + 1)], bank[:, 0:3, :])
-            else:
-                nc.scalar.copy(turned[0][u][:] if b == 0 else turned[1][:, :, P * u : P * (u + 1)], bank[:])
+            nc.scalar.copy(turned[0][u][:] if b == 0 else turned[1][:, :, P * u : P * (u + 1)], bank[:])
 
         def scatter(b, t, lo, hi, src=None):
             if src is None:
@@ -245,41 +272,55 @@ def tile_list_sponsor_slot_scores_kernel(
             for t in range(PACK if b == 0 else 1):
                 scatter(b, t, P * u, P * (u + 1))
 
-        def pick_candidates(a):
-            words = keep(f"cand{a}", [P, S2], U32)
-            nc.vector.tensor_copy(words[:], tab2[a][:].indirect(idx2[:]))
-            return words
+        def pick_candidates(a, lo, hi, slot):
+            words = keep(f"cand{a}_{lo}", [P, hi - lo], U32, slot)
+            nc.vector.tensor_copy(words[:], tab2[a][:].indirect(entries(idx2, lo, hi)))
+            for m in range(lo // P, hi // P):
+                cand[a, m] = words[:, P * m - lo : P * (m + 1) - lo]
+
+        cand = {}
 
         start(0, 0)
-        finish(0, 0)
-        start(0, 1)
         cand_sc = keep("cand_sc", [P, S2], U8)
         nc.vector.tensor_copy(cand_sc[:], tab2_sc[:].indirect(idx2[:]))
+        first_turned = []
+        for pair in range(2):
+            bank = psum.tile([P, 2, P], F32, name=f"turn_first{pair}", tag=("turn0", "A")[pair])
+            for t in range(2):
+                cols = slice(P * (2 * pair + t), P * (2 * pair + t + 1))
+                for k, part in enumerate(made[0, 0]):
+                    nc.tensor.matmul(bank[:, t, :], part[:, cols], ident[:], is_transpose=True, start=(k == 0), stop=(k == 1))
+            planes = keep(f"first_turned{pair}", [P, 2, P], F32)
+            nc.scalar.copy(planes[:], bank[:])
+            first_turned.append(planes)
+        for t in range(PACK):
+            scatter(0, t, 0, P, first_turned[t // 2][:, t % 2, :])
+        start(0, 1)
+        bank01 = turn(0, 1, *made[0, 1])
         start(0, 2)
-        finish(0, 1)
-        start(0, 3)
+        finish(0, 1, bank01)
         for a in range(2):
             w1_bf[a][1] = keep(f"w1_bf{a}1", [P, KP * PACK], BF16, ("w1_bf01", "w1_raw01")[a])[:]
             interleave(nc.scalar.copy, w1_bf[a][1], w1_raw[a][1][:])
             quantise(w1_q[a][1], w1_sc[a][1], w1_bf[a][1])
+        start(0, 3)
         finish(0, 2)
         bank03 = turn(0, 3, *made[0, 3])
-        start(1, 1)
-        cand = [pick_candidates(0)]
-        start(1, 2)
-        finish(1, 1)
         start(1, 0)
-        cand.append(pick_candidates(1))
-        last_bank = turn(1, 0, *made[1, 0])
-        start(1, 3)
+        start(1, 1)
+        bank10 = turn(1, 0, *made[1, 0])
+        pick_candidates(0, 0, S2, "cand0")
         finish(0, 3, bank03)
-        finish(1, 0, last_bank)
-        finish(1, 2)
-        finish(1, 3)
-        warm = keep("warm", [P, 1], F32, "tab0")
-        nc.scalar.activation(warm[:], turned[1][:, 0, S - 1 : S], ACT.Ln, bias=1.0, scale=0.0)
+        start(1, 2)
+        start(1, 3)
+        finish(1, 0, bank10)
+        finish(1, 1)
+        scatter(1, 1, 0, 2 * P)
+        for u in range(2, 4):
+            finish(1, u)
+            scatter(1, 1, P * u, P * (u + 1))
 
-        page_bf = [keep(f"page_bf{b}", [P, T2 * PACK], BF16, f"tab{b}") for b in range(2)]
+        page_bf = [[keep(f"page_bf0{c}", [P, KP, PACK], BF16, ("tab0", "w4_0")[c]) for c in range(2)]]
         page_q = [keep(f"page_q{b}", [P, T2], U32) for b in range(2)]
         page_sc = [keep(f"page_sc{b}", [P, T2], U8) for b in range(2)]
         joined = [keep(f"joined{c}", [P, PACK, KP], F32, f"w1_raw{c}0") for c in range(2)]
@@ -287,46 +328,72 @@ def tile_list_sponsor_slot_scores_kernel(
             for t in range(PACK):
                 nc.sync.dma_start(joined[c][:, t, :], page[0][t][:, KP * c : KP * (c + 1)])
 
+        def flat(tile_):
+            return tile_[:].rearrange("p n t -> p (n t)")
+
+        def quantise_page(b, c):
+            cols = slice(KP * c, KP * (c + 1))
+            quantise(page_q[b][:, cols], page_sc[b][:, cols], flat(page_bf[b][c]))
+
+
         def round_plane(copy, t, lo, hi):
-            copy(page_bf[1][:].rearrange("p (n t) -> p n t", t=PACK)[:, lo:hi, t], page[1][t][:, lo:hi])
+            copy(pairs_all[:, t // 2, lo:hi, t % 2], page[1][t][:, lo:hi])
+
+        def weave(copy, c):
+            words = pairs_all[:].rearrange("p h n e -> p h (n e)").bitcast(F32)[:, :, KP * c : KP * (c + 1)]
+            copy(flat(page_bf[1][c]).bitcast(F32).rearrange("p (n h) -> p n h", h=2), words.rearrange("p h n -> p n h"))
 
         score = [[None, None] for m in range(4)]
-        tags = [["gate", "A"], ["E", "B"], ["C", "D"], ["turn1", "turn0"]]
+        tags = [["gate", "B"], ["E", "D"], ["C", "A"], ["turn1", "turn0"]]
 
         def second_pass(b, m, c):
             rows = slice(P * m, P * (m + 1))
             if b == 0:
                 score[m][c] = psum.tile([P, KP], F32, name=f"score{m}{c}", tag=tags[m][c])
             nc.tensor.matmul_mx(
-                out=score[m][c][:], lhsT=cand[b][:, rows].bitcast(FP8X4), lhsT_scale=cand_sc[4 * b :, rows],
+                out=score[m][c][:], lhsT=cand[b, m].bitcast(FP8X4), lhsT_scale=cand_sc[4 * b :, rows],
                 rhs=page_q[b][:, KP * c : KP * (c + 1)].bitcast(FP8X4), rhs_scale=page_sc[b][:, KP * c : KP * (c + 1)], start=(b == 0), stop=(b == 1),
             )
 
         for c in range(2):
-            interleave(nc.scalar.copy, page_bf[0][:, KP * PACK * c : KP * PACK * (c + 1)], joined[c][:])
-        late = keep("late", [P, P], F32, "w1_raw10")
-        nc.scalar.copy(late[:], last_bank[:, 3, :])
+            interleave(nc.scalar.copy, flat(page_bf[0][c]), joined[c][:])
+        pairs_all = keep("pairs_all", [P, 2, T2, 2], BF16, "tab2_0")
+        page_bf.append([keep(f"page_bf1{c}", [P, KP, PACK], BF16) for c in range(2)])
         round_plane(nc.scalar.copy, 0, 0, T2)
-        scatter(1, 1, 0, S)
+        warm = keep("warm", [P, 1], F32)
+        nc.scalar.activation(warm[:], page[1][1][:, 0:1], ACT.Ln, bias=1.0, scale=0.0)
         round_plane(nc.scalar.copy, 1, 0, T2)
         scatter(1, 2, 0, S)
-        round_plane(nc.vector.tensor_copy, 2, 0, SPLIT)
-        round_plane(nc.scalar.copy, 2, SPLIT, T2)
-        scatter(1, 3, P, S)
-        quantise(page_q[0], page_sc[0], page_bf[0][:])
-        scatter(1, 3, 0, P, late[:])
-        round_plane(nc.vector.tensor_copy, 3, 0, SPLIT)
-        round_plane(nc.scalar.copy, 3, SPLIT, T2)
-        quantise(page_q[1], page_sc[1], page_bf[1][:])
+        round_plane(nc.scalar.copy, 2, KP, T2)
+        scatter(1, 3, 0, S)
+        for t in range(2, 4):
+            round_plane(nc.vector.tensor_copy, t, 0, KP)
+        round_plane(nc.scalar.copy, 3, KP, T2)
+        pick_candidates(1, 0, S2 // 2, "w1_raw00")
+        for c in range(2):
+            quantise_page(0, c)
+        weave(nc.vector.tensor_copy, 0)
+        weave(nc.scalar.copy, 1)
+        quantise_page(1, 0)
+        quantise_page(1, 1)
+        pick_candidates(1, S2 // 2, S2, "page_bf11")
         for m in range(4):
             for b in range(2):
                 for c in range(2):
                     second_pass(b, m, c)
+        rows = [keep(f"row{m}", [P, T2], F32, ("w4_1", "w1_bf00", "w1_bf10", "w8_0")[m]) for m in range(4)]
+        by_vector = ((0, 1), (1, 1))
+
+        def empty(copy, m, c):
+            copy(rows[m][:, KP * c : KP * (c + 1)], score[m][c][:])
+
         for m in range(4):
-            row = keep(f"row{m}", [P, T2], F32)
             for c in range(2):
-                copy = nc.scalar.copy if (m, c) in ((0, 0), (1, 0), (1, 1), (2, 0)) else nc.vector.tensor_copy
-                copy(row[:, KP * c : KP * (c + 1)], score[m][c][:])
+                if (m, c) not in by_vector:
+                    empty(nc.scalar.copy, m, c)
+        for m, row in enumerate(rows):
+            if (m, 1) in by_vector:
+                empty(nc.vector.tensor_copy, m, 1)
             pieces = 1 if m < 3 else 2
             for k in range(pieces):
                 lo, hi = NP * k // pieces, NP * (k + 1) // pieces
@@ -334,6 +401,6 @@ def tile_list_sponsor_slot_scores_kernel(
                 nc.vector.tensor_copy(unsold[:], row[:].indirect(entries(idx4, lo, hi)))
                 squared = ring.tile([P, hi - lo], F32, name="squared", tag="lin")
                 nc.scalar.activation(squared[:], unsold[:], ACT.Square, scale=budget_col[:, m : m + 1])
-                result = ring.tile([P, hi - lo], F32, name="result", tag="gated")
+                result = keep(f"result{m}{k}", [P, hi - lo], F32, f"page{k}{m}")
                 nc.scalar.activation(result[:], squared[:], ACT.Ln, bias=1.0)
                 nc.sync.dma_start(out[P * m : P * (m + 1), lo:hi], result[:])

@@ -34,7 +34,7 @@ def tile_list_sponsor_slot_scores_kernel(
         psum = ctx.enter_context(tc.psum_pool(name="psum", bufs=1))
 
         def keep(name, shape, dtype, tag=None):
-            return held.tile(shape, dtype, name=name, tag=tag or name, align_bytes=64)
+            return held.tile(shape, dtype, name=name, tag=tag or name, align_bytes=256)
 
         def entries(lst, lo, hi):
             return lst[:, lo // PER_COL : hi // PER_COL]
@@ -51,12 +51,12 @@ def tile_list_sponsor_slot_scores_kernel(
         nc.vector.memset(tab_sc[:].bitcast(I32), 0)
         ident = keep("ident", [P, P], F32)
         make_identity(nc, ident[:])
-        nc.gpsimd.memset(w4_sc[:].bitcast(I32), 0)
+        nc.vector.memset(w4_sc[:].bitcast(I32), 0)
         nc.vector.memset(w8_sc[:].bitcast(I32), 0)
         nc.vector.memset(tab2_sc[:].bitcast(I32), 0)
 
-        def load_planes_side_by_side(queue, dst, scales, quadrants):
-            for q in quadrants:
+        def load_planes_side_by_side(queue, dst, scales):
+            for q in range(4):
                 queue.dma_start(
                     dst[32 * q : 32 * q + 4, :].bitcast(I32).rearrange("r (a n) -> r a n", a=2),
                     scales[:, 4 * q : 4 * q + 4, :].bitcast(I32).rearrange("a r n -> r a n"),
@@ -101,7 +101,7 @@ def tile_list_sponsor_slot_scores_kernel(
             nc.sync.dma_start(page[b][t][:], page0.rearrange("(b p t) n -> b t p n", b=2, t=PACK)[b, t])
 
 
-        load_planes_side_by_side(nc.gpsimd, w4_sc, w4_scales, range(3))
+        load_planes_side_by_side(nc.gpsimd, tab_sc, tab_scales)
         load_planes_stacked(nc.gpsimd, tab2_sc, tab2_scales)
         wgs_rows = keep("wgs_rows", [P, S], F32)
         nc.sync.dma_start(wgs_rows[:], wgs)
@@ -110,12 +110,11 @@ def tile_list_sponsor_slot_scores_kernel(
         for dst, lst in ((idx, offs), (idx2, offs2), (idx3, offs3), (idx4, offs4)):
             nc.sync.dma_start(dst[:], lst)
         load_words(tab[0], tab_words[0])
-        load_planes_side_by_side(nc.sync, w4_sc, w4_scales, range(3, 4))
-        load_planes_side_by_side(nc.sync, tab_sc, tab_scales, range(4))
-        load_w4(0)
+        load_planes_side_by_side(nc.sync, w4_sc, w4_scales)
         load_words(tab[1], tab_words[1])
+        load_w4(0)
         load_w8(0)
-        load_planes_side_by_side(nc.sync, w8_sc, w8_scales, range(4))
+        load_planes_side_by_side(nc.sync, w8_sc, w8_scales)
         for t in range(PACK):
             load_page(0, t)
         load_w1(0, 1)
@@ -185,7 +184,7 @@ def tile_list_sponsor_slot_scores_kernel(
         made = {}
         slots = {
             ("act", 0, 0): "cand_sc", ("lin", 0, 0): "after_turn0", ("act", 0, 2): "after_turn0", ("gated", 0, 0): "after_turn1", ("lin", 0, 2): "after_turn1", ("lin", 0, 1): "w1_bf01",
-            ("act", 1, 0): "w1_raw11", ("act", 1, 1): "cand0", ("lin", 1, 0): "hold", ("lin", 1, 2): "tab0", ("lin", 1, 3): "w4_0",
+            ("act", 1, 0): "w1_raw11", ("act", 1, 1): "cand0", ("lin", 1, 0): "hold", ("lin", 1, 3): "tab0",
         }
 
         def by_plane(bank):
@@ -195,9 +194,9 @@ def tile_list_sponsor_slot_scores_kernel(
             return tile_[:].rearrange("p (t c n) -> p c t n", t=PACK, n=4)
 
         def open_banks(n):
-            gate = psum.tile([P, KP], F32, name=f"gate{n}", tag={1: "turn1", 5: "D", 7: "D"}.get(n, "gate"))
-            val = psum.tile([P, KP], F32, name=f"val{n}", tag="ACDACACA"[n])
-            skip = psum.tile([P, KP], F32, name=f"skip{n}", tag="BE"[n % 2])
+            gate = psum.tile([P, KP], F32, name=f"gate{n}", tag={1: "turn1", 5: "A", 7: "A"}.get(n, "gate"))
+            val = psum.tile([P, KP], F32, name=f"val{n}", tag="ACDACDBC"[n])
+            skip = psum.tile([P, KP], F32, name=f"skip{n}", tag="BEBEEEEE"[n])
             return gate, val, skip
 
         def product(bank, u, a, codes, scales):
@@ -207,13 +206,15 @@ def tile_list_sponsor_slot_scores_kernel(
                 rhs=codes, rhs_scale=scales, start=(a == 0), stop=(a == 1),
             )
 
-        def gate_and_val(banks, b, u, a):
+        def gate_pass(banks, b, u, a):
             product(banks[0], u, a, w4[b][:, a, :].bitcast(FP4X4), w4_sc[:, H * a + KP * b : H * a + KP * (b + 1)])
+
+        def val_pass(banks, b, u, a):
             product(banks[1], u, a, w1_q[a][b][:].bitcast(FP8X4), w1_sc[a][b][:])
 
         early = [open_banks(n) for n in range(2)]
         for u in range(2):
-            gate_and_val(early[u], 0, u, 0)
+            val_pass(early[u], 0, u, 0)
 
         def first_products(b, u):
             n = len(made)
@@ -221,8 +222,10 @@ def tile_list_sponsor_slot_scores_kernel(
                 banks = early[n]
             else:
                 banks = open_banks(n)
-                gate_and_val(banks, b, u, 0)
-            gate_and_val(banks, b, u, 1)
+                val_pass(banks, b, u, 0)
+            for a in range(2):
+                gate_pass(banks, b, u, a)
+            val_pass(banks, b, u, 1)
             gate, val, skip = banks
             for a in range(2):
                 product(skip, u, a, w8[b][:, a, :].bitcast(FP8X4), w8_sc[:, H * a + KP * b : H * a + KP * (b + 1)])
@@ -320,7 +323,7 @@ def tile_list_sponsor_slot_scores_kernel(
             finish(1, u)
             scatter(1, 1, P * u, P * (u + 1))
 
-        page_bf = [[keep(f"page_bf0{c}", [P, KP, PACK], BF16, ("tab0", "w4_0")[c]) for c in range(2)]]
+        page_bf = [[]]
         page_q = [keep(f"page_q{b}", [P, T2], U32) for b in range(2)]
         page_sc = [keep(f"page_sc{b}", [P, T2], U8) for b in range(2)]
         joined = [keep(f"joined{c}", [P, PACK, KP], F32, f"w1_raw{c}0") for c in range(2)]
@@ -344,7 +347,7 @@ def tile_list_sponsor_slot_scores_kernel(
             copy(flat(page_bf[1][c]).bitcast(F32).rearrange("p (n h) -> p n h", h=2), words.rearrange("p h n -> p n h"))
 
         score = [[None, None] for m in range(4)]
-        tags = [["gate", "B"], ["E", "D"], ["C", "A"], ["turn1", "turn0"]]
+        tags = [["gate", "A"], ["E", "D"], ["B", "C"], ["turn0", "turn1"]]
 
         def second_pass(b, m, c):
             rows = slice(P * m, P * (m + 1))
@@ -356,6 +359,7 @@ def tile_list_sponsor_slot_scores_kernel(
             )
 
         for c in range(2):
+            page_bf[0].append(keep(f"page_bf0{c}", [P, KP, PACK], BF16, ("tab0", "w1_raw00")[c]))
             interleave(nc.scalar.copy, flat(page_bf[0][c]), joined[c][:])
         pairs_all = keep("pairs_all", [P, 2, T2, 2], BF16, "tab2_0")
         page_bf.append([keep(f"page_bf1{c}", [P, KP, PACK], BF16) for c in range(2)])
@@ -369,7 +373,7 @@ def tile_list_sponsor_slot_scores_kernel(
         for t in range(2, 4):
             round_plane(nc.vector.tensor_copy, t, 0, KP)
         round_plane(nc.scalar.copy, 3, KP, T2)
-        pick_candidates(1, 0, S2 // 2, "w1_raw00")
+        pick_candidates(1, 0, S2 // 2, "w1_raw10")
         for c in range(2):
             quantise_page(0, c)
         weave(nc.vector.tensor_copy, 0)

from contextlib import ExitStack

import concourse.mybir as mybir
from concourse.masks import make_identity

K, H, T, S, T2, T3, S2, NP = 1024, 1024, 2048, 512, 1024, 2048, 512, 512
FLOPS = 2 * 3 * K * H * S + 2 * H * S2 * T2

F32 = mybir.dt.float32
BF16 = mybir.dt.bfloat16
I32 = mybir.dt.int32
U32 = mybir.dt.uint32
U16 = mybir.dt.uint16
U8 = mybir.dt.uint8
FP8X4 = mybir.dt.float8_e4m3fn_x4
FP4X4 = mybir.dt.float4_e2m1fn_x4
ACT = mybir.ActivationFunctionType
MULT = mybir.AluOpType.mult

P = 128
PACK = 4
KP = P * PACK
PER_COL = 16


def tile_list_sponsor_slot_scores_kernel(
    tc, tab_words, tab_scales, tab2_words, tab2_scales, w4_words, w4_scales,
    w8_words, w8_scales, w1, page0, wgs, budget, offs, offs2, offs3, offs4, out,
):
    nc = tc.nc
    with ExitStack() as ctx:
        held = ctx.enter_context(tc.tile_pool(name="held", bufs=1))
        ring = ctx.enter_context(tc.tile_pool(name="ring", bufs=3))
        psum = ctx.enter_context(tc.psum_pool(name="psum", bufs=1))

        def keep(name, shape, dtype, tag=None):
            return held.tile(shape, dtype, name=name, tag=tag or name, align_bytes=256)

        def entries(lst, lo, hi):
            return lst[:, lo // PER_COL : hi // PER_COL]

        idx = keep("idx", [P, S // PER_COL], U16)
        idx2 = keep("idx2", [P, S2 // PER_COL], U16)
        idx3 = keep("idx3", [P, S // PER_COL], U16)
        idx4 = keep("idx4", [P, NP // PER_COL], U16)

        tab_sc = keep("tab_sc", [P, 2 * T], U8)
        tab2_sc = keep("tab2_sc", [P, T3], U8)
        w4_sc = keep("w4_sc", [P, 2 * H], U8)
        w8_sc = keep("w8_sc", [P, 2 * H], U8)
        nc.vector.memset(tab_sc[:].bitcast(I32), 0)
        ident = keep("ident", [P, P], F32)
        make_identity(nc, ident[:])
        nc.vector.memset(w4_sc[:].bitcast(I32), 0)
        nc.vector.memset(w8_sc[:].bitcast(I32), 0)
        nc.vector.memset(tab2_sc[:].bitcast(I32), 0)

        def load_planes_side_by_side(queue, dst, scales):
            for q in range(4):
                queue.dma_start(
                    dst[32 * q : 32 * q + 4, :].bitcast(I32).rearrange("r (a n) -> r a n", a=2),
                    scales[:, 4 * q : 4 * q + 4, :].bitcast(I32).rearrange("a r n -> r a n"),
                )

        def load_planes_stacked(queue, dst, scales):
            for q in range(4):
                queue.dma_start(
                    dst[32 * q : 32 * q + 8, :].bitcast(I32),
                    scales[:, 4 * q : 4 * q + 4, :].bitcast(I32),
                )

        def load_words(dst, words):
            nc.sync.dma_start(dst[:].bitcast(I32), words.rearrange("p n i -> p (n i)").bitcast(I32))

        w1_raw = [[keep(f"w1_raw{a}{b}", [P, PACK, KP], F32) for b in range(2)] for a in range(2)]
        w4 = [keep(f"w4_{b}", [P, 2, 2 * KP], U8) for b in range(2)]
        w8 = [keep(f"w8_{b}", [P, 2, KP], U32) for b in range(2)]
        tab = [keep(f"tab{a}", [P, T], U32) for a in range(2)]
        tab2 = [keep(f"tab2_{a}", [P, T3], U32) for a in range(2)]
        page = [[keep(f"page{b}{t}", [P, T2], F32) for t in range(PACK)] for b in range(2)]
        gain = keep("gain", [P, PACK * S], F32)
        budget_col = keep("budget_col", [P, S2 // P], F32)

        def load_w1(a, b):
            rows = w1[KP * a : KP * (a + 1), KP * b : KP * (b + 1)]
            nc.sync.dma_start(w1_raw[a][b][:], rows.rearrange("(p i) c -> p i c", i=PACK))

        def load_w4(b):
            nc.sync.dma_start(
                w4[b][:].bitcast(I32),
                w4_words.rearrange("a p n -> p a n")[:, :, 2 * KP * b : 2 * KP * (b + 1)].bitcast(I32),
            )

        def load_w8(b):
            nc.sync.dma_start(
                w8[b][:].bitcast(I32),
                w8_words.rearrange("a p n i -> p a (n i)")[:, :, 4 * KP * b : 4 * KP * (b + 1)].bitcast(I32),
            )

        def load_page(b, t):
            nc.sync.dma_start(page[b][t][:], page0.rearrange("(b p t) n -> b t p n", b=2, t=PACK)[b, t])


        load_planes_side_by_side(nc.gpsimd, tab_sc, tab_scales)
        load_planes_stacked(nc.gpsimd, tab2_sc, tab2_scales)
        wgs_rows = keep("wgs_rows", [P, S], F32)
        nc.sync.dma_start(wgs_rows[:], wgs)
        load_w1(0, 0)
        load_w1(1, 0)
        for dst, lst in ((idx, offs), (idx2, offs2), (idx3, offs3), (idx4, offs4)):
            nc.sync.dma_start(dst[:], lst)
        load_words(tab[0], tab_words[0])
        load_planes_side_by_side(nc.sync, w4_sc, w4_scales)
        load_words(tab[1], tab_words[1])
        load_w4(0)
        load_w8(0)
        load_planes_side_by_side(nc.sync, w8_sc, w8_scales)
        for t in range(PACK):
            load_page(0, t)
        load_w1(0, 1)
        load_w1(1, 1)
        load_w4(1)
        load_w8(1)
        load_page(1, 0)
        load_words(tab2[0], tab2_words[0])
        load_words(tab2[1], tab2_words[1])
        for t in range(1, PACK):
            load_page(1, t)
        with nc.allow_non_contiguous_dma(reason="one budget value a partition"):
            nc.sync.dma_start(budget_col[:], budget.rearrange("(c p) -> p c", p=P))

        flipped = psum.tile([P, 4, P], F32, name="flipped", tag="gate")
        for u in range(4):
            nc.tensor.matmul(flipped[:, u, :], wgs_rows[:, P * u : P * (u + 1)], ident[:], is_transpose=True, start=True, stop=True)
        spread = [keep(f"spread{u}", [P, PACK, 4, 32], F32, f"spread{u}") for u in range(4)]
        planes = [psum.tile([P, S], F32, name=f"gain_bank{t}", tag=("turn0", "D", "E", "B")[t]) for t in range(PACK)]
        for u in range(4):
            by_slot = flipped[:, u, :].rearrange("j (q t) -> j t q", t=PACK)
            nc.scalar.copy(spread[u][:], by_slot.unsqueeze(2).to_broadcast([P, PACK, 4, 32]))
            for t in range(PACK):
                nc.tensor.matmul(
                    planes[t][:, P * u : P * (u + 1)], spread[u][:, t, :, :].rearrange("j a q -> j (a q)"), ident[:],
                    is_transpose=True, start=True, stop=True,
                )
        for t in range(PACK):
            nc.scalar.copy(gain[:, S * t : S * (t + 1)], planes[t][:])

        w1_bf = [[keep(f"w1_bf{a}0", [P, KP * PACK], BF16)[:], None] for a in range(2)]
        w1_q = [[keep(f"w1_q{a}{b}", [P, KP], U32) for b in range(2)] for a in range(2)]
        w1_sc = [[keep(f"w1_sc{a}{b}", [P, KP], U8) for b in range(2)] for a in range(2)]

        def interleave(copy, dst, src):
            copy(dst.rearrange("p (c n i) -> p c i n", n=4, i=PACK), src.rearrange("p i (c n) -> p c i n", n=4))

        def quantise(codes, scales, values):
            nc.vector.quantize_mx(out=codes[:].bitcast(FP8X4), scales=scales[:], in_=values)

        picked = [keep(f"picked{a}", [P, S], U32) for a in range(2)]
        picked_sc = {}

        def pick_scales(a, lo, hi, dst):
            picked_sc[a, lo] = dst
            nc.vector.tensor_copy(dst, tab_sc[:, T * a : T * (a + 1)].indirect(entries(idx, lo, hi)))

        def pick_words(a, lo, hi):
            nc.vector.tensor_copy(picked[a][:, lo:hi], tab[a][:].indirect(entries(idx, lo, hi)))

        half = S // 2
        for a in range(2):
            interleave(nc.vector.tensor_copy, w1_bf[a][0], w1_raw[a][0][:])
        for a in range(2):
            quantise(w1_q[a][0], w1_sc[a][0], w1_bf[a][0])
        pick_words(0, 0, half)
        for a in range(2):
            pick_scales(a, 0, half, keep(f"picked_sc{a}", [P, half], U8)[:])
        pick_words(0, half, S)
        pick_words(1, 0, half)
        pick_words(1, half, S)
        later_sc = keep("later_sc", [P, S], U8, "tab1")
        for a in range(2):
            pick_scales(a, half, S, later_sc[:, half * a : half * (a + 1)])

        turned = [{}, keep("turned1", [P, PACK, S], F32)]
        made = {}
        slots = {
            ("act", 0, 0): "cand_sc", ("lin", 0, 0): "after_turn0", ("act", 0, 2): "after_turn0", ("gated", 0, 0): "after_turn1", ("lin", 0, 2): "after_turn1", ("lin", 0, 1): "w1_bf01",
            ("act", 1, 0): "w1_raw11", ("act", 1, 1): "cand0", ("lin", 1, 0): "hold", ("lin", 1, 3): "tab0",
        }

        def by_plane(bank):
            return bank[:].rearrange("p (c n t) -> p c t n", n=4, t=PACK)

        def as_planes(tile_):
            return tile_[:].rearrange("p (t c n) -> p c t n", t=PACK, n=4)

        def open_banks(n):
            gate = psum.tile([P, KP], F32, name=f"gate{n}", tag={1: "turn1", 5: "A", 7: "A"}.get(n, "gate"))
            val = psum.tile([P, KP], F32, name=f"val{n}", tag="ACDACDBC"[n])
            skip = psum.tile([P, KP], F32, name=f"skip{n}", tag="BEBEEEEE"[n])
            return gate, val, skip

        def product(bank, u, a, codes, scales):
            cols = slice(P * u, P * (u + 1))
            nc.tensor.matmul_mx(
                out=bank[:], lhsT=picked[a][:, cols].bitcast(FP8X4), lhsT_scale=picked_sc[a, u // 2 * half][:, P * (u % 2) : P * (u % 2 + 1)],
                rhs=codes, rhs_scale=scales, start=(a == 0), stop=(a == 1),
            )

        def gate_pass(banks, b, u, a):
            product(banks[0], u, a, w4[b][:, a, :].bitcast(FP4X4), w4_sc[:, H * a + KP * b : H * a + KP * (b + 1)])

        def val_pass(banks, b, u, a):
            product(banks[1], u, a, w1_q[a][b][:].bitcast(FP8X4), w1_sc[a][b][:])

        early = [open_banks(n) for n in range(2)]
        for u in range(2):
            val_pass(early[u], 0, u, 0)

        def first_products(b, u):
            n = len(made)
            if n < 2:
                banks = early[n]
            else:
                banks = open_banks(n)
                val_pass(banks, b, u, 0)
            for a in range(2):
                gate_pass(banks, b, u, a)
            val_pass(banks, b, u, 1)
            gate, val, skip = banks
            for a in range(2):
                product(skip, u, a, w8[b][:, a, :].bitcast(FP8X4), w8_sc[:, H * a + KP * b : H * a + KP * (b + 1)])

            def stage(kind):
                slot = slots.get((kind, b, u))
                if slot:
                    return keep(f"{kind}{b}{u}", [P, KP], F32, slot)
                return ring.tile([P, KP], F32, name=kind, tag=kind)

            act = stage("act")
            nc.scalar.activation(as_planes(act), by_plane(gate), ACT.Silu)
            lin = stage("lin")
            nc.scalar.copy(as_planes(lin), by_plane(skip))
            gated = stage("gated")
            nc.vector.tensor_tensor(as_planes(gated), by_plane(val), as_planes(act), MULT)
            return gated, lin

        def turn(b, u, gated, lin):
            bank = psum.tile([P, PACK, P], F32, name=f"turn{b}{u}", tag=f"turn{u % 2}")
            for t in range(PACK):
                cols = slice(P * t, P * (t + 1))
                nc.tensor.matmul(bank[:, t, :], gated[:, cols], ident[:], is_transpose=True, start=True, stop=False)
                nc.tensor.matmul(bank[:, t, :], lin[:, cols], ident[:], is_transpose=True, start=False, stop=True)
            return bank

        def drain(b, u, bank):
            if b == 0:
                turned[0][u] = keep(f"turned0{u}", [P, PACK, P], F32, {2: "w1_bf01", 3: "hold"}.get(u))
            nc.scalar.copy(turned[0][u][:] if b == 0 else turned[1][:, :, P * u : P * (u + 1)], bank[:])

        def scatter(b, t, lo, hi, src=None):
            if src is None:
                src = turned[0][lo // P][:, t, :] if b == 0 else turned[1][:, t, lo:hi]
            nc.vector.tensor_tensor(
                page[b][t][:].indirect(entries(idx3, lo, hi)), src, gain[:, S * t + lo : S * t + hi], MULT,
            )


        def start(b, u):
            made[b, u] = first_products(b, u)

        def finish(b, u, bank=None):
            if bank is None:
                bank = turn(b, u, *made[b, u])
            drain(b, u, bank)
            for t in range(PACK if b == 0 else 1):
                scatter(b, t, P * u, P * (u + 1))

        def pick_candidates(a, lo, hi, slot):
            words = keep(f"cand{a}_{lo}", [P, hi - lo], U32, slot)
            nc.vector.tensor_copy(words[:], tab2[a][:].indirect(entries(idx2, lo, hi)))
            for m in range(lo // P, hi // P):
                cand[a, m] = words[:, P * m - lo : P * (m + 1) - lo]

        cand = {}

        start(0, 0)
        cand_sc = keep("cand_sc", [P, S2], U8)
        nc.vector.tensor_copy(cand_sc[:], tab2_sc[:].indirect(idx2[:]))
        first_turned = []
        for pair in range(2):
            bank = psum.tile([P, 2, P], F32, name=f"turn_first{pair}", tag=("turn0", "A")[pair])
            for t in range(2):
                cols = slice(P * (2 * pair + t), P * (2 * pair + t + 1))
                for k, part in enumerate(made[0, 0]):
                    nc.tensor.matmul(bank[:, t, :], part[:, cols], ident[:], is_transpose=True, start=(k == 0), stop=(k == 1))
            planes = keep(f"first_turned{pair}", [P, 2, P], F32)
            nc.scalar.copy(planes[:], bank[:])
            first_turned.append(planes)
        for t in range(PACK):
            scatter(0, t, 0, P, first_turned[t // 2][:, t % 2, :])
        start(0, 1)
        bank01 = turn(0, 1, *made[0, 1])
        start(0, 2)
        finish(0, 1, bank01)
        for a in range(2):
            w1_bf[a][1] = keep(f"w1_bf{a}1", [P, KP * PACK], BF16, ("w1_bf01", "w1_raw01")[a])[:]
            interleave(nc.scalar.copy, w1_bf[a][1], w1_raw[a][1][:])
            quantise(w1_q[a][1], w1_sc[a][1], w1_bf[a][1])
        start(0, 3)
        finish(0, 2)
        bank03 = turn(0, 3, *made[0, 3])
        start(1, 0)
        start(1, 1)
        bank10 = turn(1, 0, *made[1, 0])
        pick_candidates(0, 0, S2, "cand0")
        finish(0, 3, bank03)
        start(1, 2)
        start(1, 3)
        finish(1, 0, bank10)
        finish(1, 1)
        scatter(1, 1, 0, 2 * P)
        for u in range(2, 4):
            finish(1, u)
            scatter(1, 1, P * u, P * (u + 1))

        page_bf = [[]]
        page_q = [keep(f"page_q{b}", [P, T2], U32) for b in range(2)]
        page_sc = [keep(f"page_sc{b}", [P, T2], U8) for b in range(2)]
        joined = [keep(f"joined{c}", [P, PACK, KP], F32, f"w1_raw{c}0") for c in range(2)]
        for c in range(2):
            for t in range(PACK):
                nc.sync.dma_start(joined[c][:, t, :], page[0][t][:, KP * c : KP * (c + 1)])

        def flat(tile_):
            return tile_[:].rearrange("p n t -> p (n t)")

        def quantise_page(b, c):
            cols = slice(KP * c, KP * (c + 1))
            quantise(page_q[b][:, cols], page_sc[b][:, cols], flat(page_bf[b][c]))


        def round_plane(copy, t, lo, hi):
            copy(pairs_all[:, t // 2, lo:hi, t % 2], page[1][t][:, lo:hi])

        def weave(copy, c):
            words = pairs_all[:].rearrange("p h n e -> p h (n e)").bitcast(F32)[:, :, KP * c : KP * (c + 1)]
            copy(flat(page_bf[1][c]).bitcast(F32).rearrange("p (n h) -> p n h", h=2), words.rearrange("p h n -> p n h"))

        score = [[None, None] for m in range(4)]
        tags = [["gate", "A"], ["E", "D"], ["B", "C"], ["turn0", "turn1"]]

        def second_pass(b, m, c):
            rows = slice(P * m, P * (m + 1))
            if b == 0:
                score[m][c] = psum.tile([P, KP], F32, name=f"score{m}{c}", tag=tags[m][c])
            nc.tensor.matmul_mx(
                out=score[m][c][:], lhsT=cand[b, m].bitcast(FP8X4), lhsT_scale=cand_sc[4 * b :, rows],
                rhs=page_q[b][:, KP * c : KP * (c + 1)].bitcast(FP8X4), rhs_scale=page_sc[b][:, KP * c : KP * (c + 1)], start=(b == 0), stop=(b == 1),
            )

        for c in range(2):
            page_bf[0].append(keep(f"page_bf0{c}", [P, KP, PACK], BF16, ("tab0", "w1_raw00")[c]))
            interleave(nc.scalar.copy, flat(page_bf[0][c]), joined[c][:])
        pairs_all = keep("pairs_all", [P, 2, T2, 2], BF16, "tab2_0")
        page_bf.append([keep(f"page_bf1{c}", [P, KP, PACK], BF16) for c in range(2)])
        round_plane(nc.scalar.copy, 0, 0, T2)
        warm = keep("warm", [P, 1], F32)
        nc.scalar.activation(warm[:], page[1][1][:, 0:1], ACT.Ln, bias=1.0, scale=0.0)
        round_plane(nc.scalar.copy, 1, 0, T2)
        scatter(1, 2, 0, S)
        round_plane(nc.scalar.copy, 2, KP, T2)
        scatter(1, 3, 0, S)
        for t in range(2, 4):
            round_plane(nc.vector.tensor_copy, t, 0, KP)
        round_plane(nc.scalar.copy, 3, KP, T2)
        pick_candidates(1, 0, S2 // 2, "w1_raw10")
        for c in range(2):
            quantise_page(0, c)
        weave(nc.vector.tensor_copy, 0)
        weave(nc.scalar.copy, 1)
        quantise_page(1, 0)
        quantise_page(1, 1)
        pick_candidates(1, S2 // 2, S2, "page_bf11")
        for m in range(4):
            for b in range(2):
                for c in range(2):
                    second_pass(b, m, c)
        rows = [keep(f"row{m}", [P, T2], F32, ("w4_1", "w1_bf00", "w1_bf10", "w8_0")[m]) for m in range(4)]
        by_vector = ((0, 1), (1, 1))

        def empty(copy, m, c):
            copy(rows[m][:, KP * c : KP * (c + 1)], score[m][c][:])

        for m in range(4):
            for c in range(2):
                if (m, c) not in by_vector:
                    empty(nc.scalar.copy, m, c)
        for m, row in enumerate(rows):
            if (m, 1) in by_vector:
                empty(nc.vector.tensor_copy, m, 1)
            pieces = 1 if m < 3 else 2
            for k in range(pieces):
                lo, hi = NP * k // pieces, NP * (k + 1) // pieces
                unsold = ring.tile([P, hi - lo], F32, name="unsold", tag="act")
                nc.vector.tensor_copy(unsold[:], row[:].indirect(entries(idx4, lo, hi)))
                squared = ring.tile([P, hi - lo], F32, name="squared", tag="lin")
                nc.scalar.activation(squared[:], unsold[:], ACT.Square, scale=budget_col[:, m : m + 1])
                result = keep(f"result{m}{k}", [P, hi - lo], F32, f"page{k}{m}")
                nc.scalar.activation(result[:], squared[:], ACT.Ln, bias=1.0)
                nc.sync.dma_start(out[P * m : P * (m + 1), lo:hi], result[:])
